import numpy as np, ml_dtypes
CORES = [10,14,66,70,74,78,82,86,90,94,106,110]
N = 12
DEG, TK = 4, 256
MASK = [[0,5,6,7],[0,1,4,5],[2,3,7,10],[2,3,4,6],[3,4,6,11],[1,2,5,8],[1,6,7,11],[1,4,7,9],[1,3,4,8],[0,5,8,9],[1,5,9,10],[1,5,6,11]]
def setup_inputs(rng):
    return {"x": rng.standard_normal((N, 128, TK), dtype=np.float32).astype(ml_dtypes.bfloat16), "w": rng.standard_normal((N, 128, DEG * 128), dtype=np.float32).astype(ml_dtypes.bfloat16)}
def setup_inputs_big(rng):
    d = setup_inputs(rng)
    for k in ("x", "w"): d[k] = (d[k].astype(np.float32) * 1024.0).astype(d[k].dtype)
    return d
def setup_inputs_small(rng):
    d = setup_inputs(rng)
    for k in ("x", "w"): d[k] = (d[k].astype(np.float32) * (1 / 1024.0)).astype(d[k].dtype)
    return d
def setup_inputs_apart(rng):
    d = setup_inputs(rng)
    f = (10.0 ** rng.permutation(np.linspace(-1.5, 1.5, N))).astype(np.float32).reshape(N, 1, 1)
    for k in ("x", "w"): d[k] = (d[k].astype(np.float32) * f).astype(d[k].dtype)
    return d
def reference(x, w):
    X, W = x.astype(np.float64), w.astype(np.float64)
    y = np.zeros((N, 128, TK))
    for r in range(N):
        for i, j in enumerate(MASK[r]):
            y[r] += W[r][:, 128 * i:128 * i + 128].T @ X[j]
    return {"y": y.astype(ml_dtypes.bfloat16 if x.dtype != np.float64 else np.float64)}

from concourse.bass import DstId, RemoteDMATransfer

TK = 256
TM = 128
DEG = 4
NR = 12
KEEP = 99

SCRATCH = {
    "xb0": ("sbuf", [128, TK], "bfloat16"),
    "xb1": ("sbuf", [128, TK], "bfloat16"),
    "xb2": ("sbuf", [128, TK], "bfloat16"),
    "xb3": ("sbuf", [128, TK], "bfloat16"),
    "ws": ("sbuf", [128, DEG * TM], "bfloat16"),
    "ys": ("sbuf", [128, TK], "bfloat16"),
    "acc": ("psum", [128, TK], "float32"),
}
SEMAPHORES = ["xl", "wl", "sent", "mm", "cp", "st"] + ["s%d" % j for j in range(NR)]
if KEEP < DEG:
    SCRATCH["xd"] = ("dram", [128, TK], "bfloat16")
    for _i in range(DEG):
        SCRATCH["ld%d" % _i] = ("dram", [128, TK], "bfloat16")
    SEMAPHORES += ["xdl"] + ["l%d" % _i for _i in range(DEG)]

_CACHE = {}


def _bits(m):
    return [b for b in range(m.bit_length()) if (m >> b) & 1]


def _perms(items):
    if len(items) <= 1:
        return [list(items)]
    return [[items[k]] + p for k in range(len(items)) for p in _perms(items[:k] + items[k + 1:])]


def _links(topo, s, d):
    cs, cd, di = topo.chip(s), topo.chip(d), topo.die(s)
    if cs == cd:
        return []
    out, at = [], cs
    if not topo.same_plane(cs, cd):
        out.append(("mate", cs, di))
        if topo.mates(cs, cd):
            return out
        at = [c for c in range(topo.CHIPS) if topo.mates(cs, c)][0]
    return out + [("out", at, di), ("in", cd, di)]


def _plan(cores, mask, topo):
    n = len(cores)
    chip = [topo.chip(c) for c in cores]
    groups = []
    for j in range(n):
        grp = {}
        for r in range(n):
            if j in mask[r] and r != j:
                grp.setdefault(chip[r], []).append(r)
        groups.append(grp)
    load = [sum(len(rs) if ch == chip[j] else 1 for ch, rs in groups[j].items()) for j in range(n)]
    nfwd = [0] * n
    first = [[] for _ in range(n)]
    rest = [[] for _ in range(n)]
    near = [[] for _ in range(n)]
    fwd = [[] for _ in range(n)]
    for j in range(n):
        for ch, rs in sorted(groups[j].items()):
            if ch == chip[j]:
                near[j] += rs
            elif len(rs) > 1:
                h = min(rs, key=lambda r: (nfwd[r], load[r], r))
                nfwd[h] += 1
                load[h] += len(rs) - 1
                first[j].append(h)
                fwd[h].append((j, [r for r in rs if r != h]))
            else:
                rest[j] += rs

    def cost(order):
        use = {}
        for j in range(n):
            for p, r in enumerate(order[j]):
                for k in _links(topo, cores[j], cores[r]) + [("core", r)]:
                    use[(k, p)] = use.get((k, p), 0) + 1
        return sum((v - 1) * (kp[1] + 1) * (1 if kp[0][0] == "core" else 2) for kp, v in use.items())

    def with_order(order, j, c):
        return order[:j] + [c] + order[j + 1:]

    order = [first[j] + rest[j] for j in range(n)]
    changed = True
    while changed:
        changed = False
        for j in sorted(range(n), key=lambda j: (-len(order[j]), j)):
            cands = [a + b for a in _perms(first[j]) for b in _perms(rest[j])]
            best = min(cands, key=lambda c: (cost(with_order(order, j, c)), c))
            if cost(with_order(order, j, best)) < cost(order):
                order = with_order(order, j, best)
                changed = True

    calls = [[] for _ in range(n)]
    arrive = [{} for _ in range(n)]
    used = [0] * n
    for j in range(n):
        far = 0
        if order[j]:
            far = topo.mask(cores[j], cores[order[j][0]])
            for r in order[j]:
                far &= topo.mask(cores[j], cores[r])
            nd = max(0, len(order[j]) - KEEP)
            if nd:
                calls[j].append((j, order[j][:nd], far, False, True))
            calls[j].append((j, order[j][nd:], far, False, False))
            for p, r in enumerate(order[j]):
                arrive[r][j] = (len(_bits(far)), p + (3.0 if p < nd else 1.0), p < nd)
        used[j] |= far
        for p, r in enumerate(near[j]):
            m = topo.mask(cores[j], cores[r])
            if len(_bits(m & ~far)) in (1, 2, 4, 8, 16):
                m = m & ~far
            calls[j].append((j, [r], m, False, False))
            arrive[r][j] = (len(_bits(m)), p + 1.5, False)
            used[j] |= m
    for h in range(n):
        for j, rs in sorted(fwd[h], key=lambda e: arrive[h][e[0]][1]):
            m = topo.mask(cores[h], cores[rs[0]])
            for r in rs:
                m &= topo.mask(cores[h], cores[r])
            if len(_bits(m & used[h])) in (1, 2, 4, 8, 16):
                m = m & used[h]
            calls[h].append((j, rs, m, True, False))
            for p, r in enumerate(rs):
                arrive[r][j] = (len(_bits(m)), order[j].index(h) + 3.0 + p, False)
    return calls, arrive


def rank_program(g, core, T, topo):
    rank = T.rank_of(core)
    if rank is None:
        return
    cores, mask = list(T.cores), T.tables["MASK"]
    if "plan" not in _CACHE:
        _CACHE["plan"] = _plan(cores, mask, topo)
    calls, arrive = _CACHE["plan"]
    mine = mask[rank]
    S = T.sem

    g.sync.dma_start(T["xb%d" % mine.index(rank)][:, :], T.x[:, :]).then_inc(S.xl, 16)
    g.sync.dma_start(T.ws[:, :], T.w[:, :]).then_inc(S.wl, 16)
    if any(c[4] for c in calls[rank]):
        g.scalar.dma_start(T.xd[:, :], T.x[:, :]).then_inc(S.xdl, 16)

    total = 0
    waited = set()
    for j, rs, m, passes, to_dram in calls[rank]:
        i = mine.index(j)
        if passes:
            g.wait_ge(S["s%d" % j], arrive[rank][j][0])
            src = T["ld%d" % i] if arrive[rank][j][2] else T["xb%d" % i]
        else:
            src, sem = (T.xd, S.xdl) if to_dram else (T["xb%d" % i], S.xl)
            if to_dram not in waited:
                g.wait_ge(sem, 16)
                waited.add(to_dram)
        ids = []
        for r in rs:
            rid, pid, _se = topo.addr(cores[r])
            ids.append(DstId(rid=rid, pnc=pid))
        g.remote_dma_fused([RemoteDMATransfer(
            dst_ids=ids, dma_engine_mask=m, remote_sem=S["s%d" % j], srcs=[src[:, :]],
            dsts=[T[("ld%d" if to_dram else "xb%d") % mask[r].index(j)][:, :] for r in rs], alu_op=0)],
            local_sem=S.sent)
        total += len(_bits(m))
    g.wait_ge(S.sent, total)

    seq = [rank] + sorted([j for j in mine if j != rank], key=lambda j: (arrive[rank][j][1], j))

    for j in seq[1:]:
        if arrive[rank][j][2]:
            i = mine.index(j)
            g.scalar.wait_ge(S["s%d" % j], arrive[rank][j][0])
            g.scalar.dma_start(T["xb%d" % i][:, :], T["ld%d" % i][:, :]).then_inc(S["l%d" % i], 16)

    g.tensor.wait_ge(S.wl, 16)
    g.tensor.wait_ge(S.xl, 16)
    for k, j in enumerate(seq):
        i = mine.index(j)
        if j != rank:
            if arrive[rank][j][2]:
                g.tensor.wait_ge(S["l%d" % i], 16)
            else:
                g.tensor.wait_ge(S["s%d" % j], arrive[rank][j][0])
        mmi = g.tensor.matmul(T.acc[:, :], T.ws[:, TM * i:TM * (i + 1)], T["xb%d" % i][:, :],
                              start=(k == 0), stop=(k == DEG - 1))
        if k == DEG - 1:
            mmi.then_inc(S.mm, 1)

    g.vector.wait_ge(S.mm, 1)
    g.vector.tensor_copy(T.ys[:, :], T.acc[:, :]).then_inc(S.cp, 1)
    g.sync.wait_ge(S.cp, 1)
    g.sync.dma_start(T.y[:, :], T.ys[:, :]).then_inc(S.st, 16)
    g.sync.wait_ge(S.st, 16)
